import numpy as np
CORES = [40,41,42,43,44,45,46,47,208,209,210,211,212,213,214,215]
N = 16
GROUPS = [[0,1,2,3,4,5,6,7],[8,9,10,11,12,13,14,15]]
def setup_inputs(rng):
    return {"x": rng.standard_normal((N, 128, 512), dtype=np.float32)}
def reference(x):
    y = np.empty((N, 128, 64), x.dtype)
    for g in GROUPS:
        s = x[g].sum(axis=0, dtype=np.float64).astype(x[g].dtype)
        n = len(g); b = x.shape[2] // n
        for i, r in enumerate(g):
            y[r] = s[:, i * b:(i + 1) * b]
    return {"y": y}

@@ -1,0 +1,57 @@
+from concourse.bass import DstId, RemoteDMATransfer
+
+C = 4
+NM = 8
+
+SCRATCH = {
+    "xh":   ("dram", [NM, 128, 64], "float32"),
+    "cont": ("dram", [NM - 1, 128, 64], "float32"),
+    "land": ("dram", [C, 128, 64], "float32"),
+}
+SEMAPHORES = ["ld", "arr", "res", "sent", "st"]
+
+
+def rank_program(g, core, T, topo):
+    rank = T.rank_of(core)
+    if rank is None:
+        return
+    grp = [m for m in T.tables["GROUPS"] if rank in m][0]
+    cores = [T.cores[r] for r in grp]
+    me = grp.index(rank)
+
+    def did(member):
+        rid, pid = topo.addr(cores[member], core)
+        return DstId(rid=rid, pnc=pid)
+
+    w = 64 * C
+    nq = NM // C
+    for q in range(nq):
+        eng = g.sync if q % 2 == 0 else g.scalar
+        eng.dma_start(T.xh[C * q:C * (q + 1)], T.x[:, w * q:w * (q + 1)]).then_inc(T.sem.ld, 16)
+    g.wait_ge(T.sem.ld, 16 * nq)
+
+    mine = me ^ C
+    tr = []
+    for s in range(NM):
+        if s == mine:
+            continue
+        k = s ^ C
+        at = me if me < k else me - 1
+        tr.append(RemoteDMATransfer(dst_ids=[did(k)], dma_engine_mask=0b11 << (2 * len(tr)), remote_sem=T.sem.arr,
+                                    src=T.xh[s], dst=T.cont[at]))
+    g.remote_dma_fused(tr, local_sem=T.sem.sent)
+
+    g.wait_ge(T.sem.arr, 2 * (NM - 1))
+    q = mine // C
+    owners = list(range(C * q, C * (q + 1)))
+    g.remote_dma_fused([RemoteDMATransfer(dst_ids=[did(j) for j in owners], dma_engine_mask=0xFFFF,
+                                          remote_sem=T.sem.res,
+                                          srcs=[T.xh[mine]] + [T.cont[i] for i in range(NM - 1)],
+                                          dsts=[T.land[mine % C] for j in owners], alu_op=1)],
+                       local_sem=T.sem.sent)
+
+    g.sync.wait_ge(T.sem.res, 16 * C)
+    g.sync.dma_start(T.y[:, :], T.land[:, (me % C)::C, :]).then_inc(T.sem.st, 16)
+
+    g.wait_ge(T.sem.sent, 2 * (NM - 1) + 16)
+    g.wait_ge(T.sem.st, 16)

@@ -1,6 +1,6 @@
 from concourse.bass import DstId, RemoteDMATransfer
 
-C = 4
+C = 2
 NM = 8
 
 SCRATCH = {

@@ -1,6 +1,6 @@
 from concourse.bass import DstId, RemoteDMATransfer
 
-C = 2
+C = 1
 NM = 8
 
 SCRATCH = {

@@ -1,14 +1,13 @@
 from concourse.bass import DstId, RemoteDMATransfer
 
-C = 1
 NM = 8
 
 SCRATCH = {
     "xh":   ("dram", [NM, 128, 64], "float32"),
     "cont": ("dram", [NM - 1, 128, 64], "float32"),
-    "land": ("dram", [C, 128, 64], "float32"),
+    "land": ("dram", [128, 64], "float32"),
 }
-SEMAPHORES = ["ld", "arr", "res", "sent", "st"]
+SEMAPHORES = ["lda", "ldb", "ldo", "arr", "res", "sent", "st"]
 
 
 def rank_program(g, core, T, topo):
@@ -18,40 +17,43 @@ def rank_program(g, core, T, topo):
     grp = [m for m in T.tables["GROUPS"] if rank in m][0]
     cores = [T.cores[r] for r in grp]
     me = grp.index(rank)
+    mine = me ^ 1
 
     def did(member):
         rid, pid = topo.addr(cores[member], core)
         return DstId(rid=rid, pnc=pid)
 
-    w = 64 * C
-    nq = NM // C
-    for q in range(nq):
-        eng = g.sync if q % 2 == 0 else g.scalar
-        eng.dma_start(T.xh[C * q:C * (q + 1)], T.x[:, w * q:w * (q + 1)]).then_inc(T.sem.ld, 16)
-    g.wait_ge(T.sem.ld, 16 * nq)
+    far = [s for s in range(NM) if topo.die(cores[s ^ 1]) != topo.die(core)]
+    near = [s for s in range(NM) if s not in far and s != mine]
 
-    mine = me ^ C
-    tr = []
-    for s in range(NM):
-        if s == mine:
-            continue
-        k = s ^ C
-        at = me if me < k else me - 1
-        tr.append(RemoteDMATransfer(dst_ids=[did(k)], dma_engine_mask=0b11 << (2 * len(tr)), remote_sem=T.sem.arr,
-                                    src=T.xh[s], dst=T.cont[at]))
-    g.remote_dma_fused(tr, local_sem=T.sem.sent)
+    plan = [(s, T.sem.lda) for s in far] + [(s, T.sem.ldb) for s in near] + [(mine, T.sem.ldo)]
+    for n, (s, sem) in enumerate(plan):
+        eng = g.sync if n % 2 == 0 else g.scalar
+        eng.dma_start(T.xh[s], T.x[:, 64 * s:64 * (s + 1)]).then_inc(sem, 16)
 
-    g.wait_ge(T.sem.arr, 2 * (NM - 1))
-    q = mine // C
-    owners = list(range(C * q, C * (q + 1)))
-    g.remote_dma_fused([RemoteDMATransfer(dst_ids=[did(j) for j in owners], dma_engine_mask=0xFFFF,
-                                          remote_sem=T.sem.res,
+    def spread(slots):
+        tr = []
+        for s in slots:
+            k = s ^ 1
+            at = me if me < k else me - 1
+            tr.append(RemoteDMATransfer(dst_ids=[did(k)], dma_engine_mask=0b1111 << (4 * len(tr)),
+                                        remote_sem=T.sem.arr, src=T.xh[s], dst=T.cont[at]))
+        g.remote_dma_fused(tr, local_sem=T.sem.sent)
+
+    g.wait_ge(T.sem.lda, 16 * len(far))
+    spread(far)
+    g.wait_ge(T.sem.ldb, 16 * len(near))
+    spread(near)
+
+    g.wait_ge(T.sem.ldo, 16)
+    g.wait_ge(T.sem.arr, 4 * (NM - 1))
+    g.remote_dma_fused([RemoteDMATransfer(dst_ids=[did(mine)], dma_engine_mask=0xFFFF, remote_sem=T.sem.res,
                                           srcs=[T.xh[mine]] + [T.cont[i] for i in range(NM - 1)],
-                                          dsts=[T.land[mine % C] for j in owners], alu_op=1)],
+                                          dsts=[T.land[:, :]], alu_op=1)],
                        local_sem=T.sem.sent)
 
-    g.sync.wait_ge(T.sem.res, 16 * C)
-    g.sync.dma_start(T.y[:, :], T.land[:, (me % C)::C, :]).then_inc(T.sem.st, 16)
+    g.sync.wait_ge(T.sem.res, 16)
+    g.sync.dma_start(T.y[:, :], T.land[:, :]).then_inc(T.sem.st, 16)
 
-    g.wait_ge(T.sem.sent, 2 * (NM - 1) + 16)
+    g.wait_ge(T.sem.sent, 4 * (NM - 1) + 16)
     g.wait_ge(T.sem.st, 16)

@@ -1,13 +1,15 @@
 from concourse.bass import DstId, RemoteDMATransfer
 
 NM = 8
+WAVES = (2, 2, 2, 1)
+ENGS = (8, 8, 8, 16)
 
 SCRATCH = {
     "xh":   ("dram", [NM, 128, 64], "float32"),
     "cont": ("dram", [NM - 1, 128, 64], "float32"),
     "land": ("dram", [128, 64], "float32"),
 }
-SEMAPHORES = ["lda", "ldb", "ldo", "arr", "res", "sent", "st"]
+SEMAPHORES = ["ld%d" % i for i in range(len(WAVES))] + ["ldo", "arr", "res", "sent", "st"]
 
 
 def rank_program(g, core, T, topo):
@@ -25,28 +27,44 @@ def rank_program(g, core, T, topo):
 
     far = [s for s in range(NM) if topo.die(cores[s ^ 1]) != topo.die(core)]
     near = [s for s in range(NM) if s not in far and s != mine]
+    order = far + near
+    waves = []
+    for n in WAVES:
+        waves.append(order[:n])
+        order = order[n:]
 
-    plan = [(s, T.sem.lda) for s in far] + [(s, T.sem.ldb) for s in near] + [(mine, T.sem.ldo)]
+    plan = [(s, T.sem["ld%d" % i]) for i, wv in enumerate(waves) for s in wv] + [(mine, T.sem.ldo)]
     for n, (s, sem) in enumerate(plan):
         eng = g.sync if n % 2 == 0 else g.scalar
         eng.dma_start(T.xh[s], T.x[:, 64 * s:64 * (s + 1)]).then_inc(sem, 16)
 
-    def spread(slots):
+    for i, wv in enumerate(waves):
+        ne = ENGS[i]
         tr = []
-        for s in slots:
+        for s in wv:
             k = s ^ 1
             at = me if me < k else me - 1
-            tr.append(RemoteDMATransfer(dst_ids=[did(k)], dma_engine_mask=0b1111 << (4 * len(tr)),
+            tr.append(RemoteDMATransfer(dst_ids=[did(k)], dma_engine_mask=((1 << ne) - 1) << (ne * len(tr)),
                                         remote_sem=T.sem.arr, src=T.xh[s], dst=T.cont[at]))
+        g.wait_ge(T.sem["ld%d" % i], 16 * len(wv))
         g.remote_dma_fused(tr, local_sem=T.sem.sent)
+    sent = sum(n * e for n, e in zip(WAVES, ENGS))
 
-    g.wait_ge(T.sem.lda, 16 * len(far))
-    spread(far)
-    g.wait_ge(T.sem.ldb, 16 * len(near))
-    spread(near)
+    arrive = 0
+    for m in range(NM):
+        if m == me:
+            continue
+        f = [s for s in range(NM) if topo.die(cores[s ^ 1]) != topo.die(cores[m])]
+        o = f + [s for s in range(NM) if s not in f and s != (m ^ 1)]
+        pos = o.index(mine)
+        for n, e in zip(WAVES, ENGS):
+            if pos < n:
+                arrive += e
+                break
+            pos -= n
 
     g.wait_ge(T.sem.ldo, 16)
-    g.wait_ge(T.sem.arr, 4 * (NM - 1))
+    g.wait_ge(T.sem.arr, arrive)
     g.remote_dma_fused([RemoteDMATransfer(dst_ids=[did(mine)], dma_engine_mask=0xFFFF, remote_sem=T.sem.res,
                                           srcs=[T.xh[mine]] + [T.cont[i] for i in range(NM - 1)],
                                           dsts=[T.land[:, :]], alu_op=1)],
@@ -55,5 +73,5 @@ def rank_program(g, core, T, topo):
     g.sync.wait_ge(T.sem.res, 16)
     g.sync.dma_start(T.y[:, :], T.land[:, :]).then_inc(T.sem.st, 16)
 
-    g.wait_ge(T.sem.sent, 4 * (NM - 1) + 16)
+    g.wait_ge(T.sem.sent, sent + 16)
     g.wait_ge(T.sem.st, 16)

@@ -1,6 +1,7 @@
 from concourse.bass import DstId, RemoteDMATransfer
 
 NM = 8
+HD = 4
 WAVES = (2, 2, 2, 1)
 ENGS = (8, 8, 8, 16)
 
@@ -10,6 +11,12 @@ SCRATCH = {
     "land": ("dram", [128, 64], "float32"),
 }
 SEMAPHORES = ["ld%d" % i for i in range(len(WAVES))] + ["ldo", "arr", "res", "sent", "st"]
+
+
+def receivers(m):
+    base, p = HD * (m // HD), m % HD
+    other = HD - base
+    return [other + (p + t) % HD for t in range(HD)] + [base + (p + t) % HD for t in range(1, HD)]
 
 
 def rank_program(g, core, T, topo):
@@ -25,15 +32,13 @@ def rank_program(g, core, T, topo):
         rid, pid = topo.addr(cores[member], core)
         return DstId(rid=rid, pnc=pid)
 
-    far = [s for s in range(NM) if topo.die(cores[s ^ 1]) != topo.die(core)]
-    near = [s for s in range(NM) if s not in far and s != mine]
-    order = far + near
+    order = receivers(me)
     waves = []
     for n in WAVES:
         waves.append(order[:n])
         order = order[n:]
 
-    plan = [(s, T.sem["ld%d" % i]) for i, wv in enumerate(waves) for s in wv] + [(mine, T.sem.ldo)]
+    plan = [(k ^ 1, T.sem["ld%d" % i]) for i, wv in enumerate(waves) for k in wv] + [(mine, T.sem.ldo)]
     for n, (s, sem) in enumerate(plan):
         eng = g.sync if n % 2 == 0 else g.scalar
         eng.dma_start(T.xh[s], T.x[:, 64 * s:64 * (s + 1)]).then_inc(sem, 16)
@@ -41,11 +46,10 @@ def rank_program(g, core, T, topo):
     for i, wv in enumerate(waves):
         ne = ENGS[i]
         tr = []
-        for s in wv:
-            k = s ^ 1
+        for k in wv:
             at = me if me < k else me - 1
             tr.append(RemoteDMATransfer(dst_ids=[did(k)], dma_engine_mask=((1 << ne) - 1) << (ne * len(tr)),
-                                        remote_sem=T.sem.arr, src=T.xh[s], dst=T.cont[at]))
+                                        remote_sem=T.sem.arr, src=T.xh[k ^ 1], dst=T.cont[at]))
         g.wait_ge(T.sem["ld%d" % i], 16 * len(wv))
         g.remote_dma_fused(tr, local_sem=T.sem.sent)
     sent = sum(n * e for n, e in zip(WAVES, ENGS))
@@ -54,9 +58,7 @@ def rank_program(g, core, T, topo):
     for m in range(NM):
         if m == me:
             continue
-        f = [s for s in range(NM) if topo.die(cores[s ^ 1]) != topo.die(cores[m])]
-        o = f + [s for s in range(NM) if s not in f and s != (m ^ 1)]
-        pos = o.index(mine)
+        pos = receivers(m).index(me)
         for n, e in zip(WAVES, ENGS):
             if pos < n:
                 arrive += e

from concourse.bass import DstId, RemoteDMATransfer

NM = 8
HD = 4
WAVES = (2, 2, 2, 1)
ENGS = (8, 8, 8, 16)

SCRATCH = {
    "xh":   ("dram", [NM, 128, 64], "float32"),
    "cont": ("dram", [NM - 1, 128, 64], "float32"),
    "land": ("dram", [128, 64], "float32"),
}
SEMAPHORES = ["ld%d" % i for i in range(len(WAVES))] + ["ldo", "arr", "res", "sent", "st"]


def receivers(m):
    base, p = HD * (m // HD), m % HD
    other = HD - base
    return [other + (p + t) % HD for t in range(HD)] + [base + (p + t) % HD for t in range(1, HD)]


def rank_program(g, core, T, topo):
    rank = T.rank_of(core)
    if rank is None:
        return
    grp = [m for m in T.tables["GROUPS"] if rank in m][0]
    cores = [T.cores[r] for r in grp]
    me = grp.index(rank)
    mine = me ^ 1

    def did(member):
        rid, pid = topo.addr(cores[member], core)
        return DstId(rid=rid, pnc=pid)

    order = receivers(me)
    waves = []
    for n in WAVES:
        waves.append(order[:n])
        order = order[n:]

    plan = [(k ^ 1, T.sem["ld%d" % i]) for i, wv in enumerate(waves) for k in wv] + [(mine, T.sem.ldo)]
    for n, (s, sem) in enumerate(plan):
        eng = g.sync if n % 2 == 0 else g.scalar
        eng.dma_start(T.xh[s], T.x[:, 64 * s:64 * (s + 1)]).then_inc(sem, 16)

    for i, wv in enumerate(waves):
        ne = ENGS[i]
        tr = []
        for k in wv:
            at = me if me < k else me - 1
            tr.append(RemoteDMATransfer(dst_ids=[did(k)], dma_engine_mask=((1 << ne) - 1) << (ne * len(tr)),
                                        remote_sem=T.sem.arr, src=T.xh[k ^ 1], dst=T.cont[at]))
        g.wait_ge(T.sem["ld%d" % i], 16 * len(wv))
        g.remote_dma_fused(tr, local_sem=T.sem.sent)
    sent = sum(n * e for n, e in zip(WAVES, ENGS))

    arrive = 0
    for m in range(NM):
        if m == me:
            continue
        pos = receivers(m).index(me)
        for n, e in zip(WAVES, ENGS):
            if pos < n:
                arrive += e
                break
            pos -= n

    g.wait_ge(T.sem.ldo, 16)
    g.wait_ge(T.sem.arr, arrive)
    g.remote_dma_fused([RemoteDMATransfer(dst_ids=[did(mine)], dma_engine_mask=0xFFFF, remote_sem=T.sem.res,
                                          srcs=[T.xh[mine]] + [T.cont[i] for i in range(NM - 1)],
                                          dsts=[T.land[:, :]], alu_op=1)],
                       local_sem=T.sem.sent)

    g.sync.wait_ge(T.sem.res, 16)
    g.sync.dma_start(T.y[:, :], T.land[:, :]).then_inc(T.sem.st, 16)

    g.wait_ge(T.sem.sent, sent + 16)
    g.wait_ge(T.sem.st, 16)
